import numpy as np
import ml_dtypes


def mxq(x, axis, fmt="e4m3"):
    dtype, down = {"e4m3": (ml_dtypes.float8_e4m3fn, 7), "e5m2": (ml_dtypes.float8_e5m2, 14)}[fmt]
    v = np.moveaxis(np.asarray(x, np.float32).astype(ml_dtypes.bfloat16).astype(np.float64), axis, -1)
    blocks = v.reshape(v.shape[:-1] + (-1, 32))
    amax = np.abs(blocks).max(-1, keepdims=True)
    byte = np.maximum(np.where(amax > 0, np.frexp(amax)[1] - 1 + 127, 0) - down, 1)
    scale = np.exp2(byte - 127.0)
    codes = (blocks / scale).astype(np.float32).astype(dtype).astype(np.float64)
    return np.moveaxis((codes * scale).reshape(v.shape), -1, axis)


WIDE = False


def mx_kscale(k):
    if not WIDE:
        return np.ones(k)
    levels = np.array([10, -10, 5, -5, 0])
    if k % 512:
        return np.exp2(np.random.permutation(np.resize(levels, k // 32))).repeat(32)
    a = np.empty((k // 512, 16))
    for p in range(k // 512):
        a[p, :8] = np.random.permutation(np.resize(levels, 8))
        for g in range(8):
            far = levels[np.abs(levels - a[p, g]) >= 10]
            a[p, g + 8] = far[np.random.randint(len(far))]
    return np.exp2(a.ravel()).repeat(32)


def f64(x):
    return np.asarray(x).astype(np.float64)


def striped(idx):
    return np.tile(idx.reshape(-1, 16).T, (8, 1)).astype(np.uint16)


def unstriped(offs):
    return offs[:16].T.reshape(-1).astype(np.int64)


E2M1 = np.array([0.0, 0.5, 1.0, 1.5, 2.0, 3.0, 4.0, 6.0, -0.0, -0.5, -1.0, -1.5, -2.0, -3.0, -4.0, -6.0])


def pack_weight(w, fmt):
    k, n = w.shape
    w = f64(np.asarray(w, np.float32).astype(ml_dtypes.bfloat16)).reshape(k // 32, 32, n)
    amax = np.abs(w).max(1)
    if fmt == "e4m3":
        byte = np.frexp(amax)[1] - 1 + 127 - 7
    else:
        mant, ex = np.frexp(amax / 6.0)
        byte = np.where(mant > 0.5, ex, ex - 1) + 127
    byte = np.clip(np.where(amax > 0, byte, 1), 1, 254)
    scaled = (w * np.exp2(127.0 - byte)[:, None, :]).reshape(k, n).astype(np.float32)
    by_word = np.ascontiguousarray(scaled.reshape(k // 512, 128, 4, n).transpose(0, 1, 3, 2))
    if fmt == "e4m3":
        words = by_word.astype(ml_dtypes.float8_e4m3fn).view(np.uint8)
    else:
        c = by_word.astype(ml_dtypes.float4_e2m1fn).view(np.uint8) & 0xF
        words = (c[..., 0::2] | (c[..., 1::2] << 4)).reshape(k // 512, 128, 2 * n)
    return np.ascontiguousarray(words), np.ascontiguousarray(byte.astype(np.uint8).reshape(k // 512, 16, n))


def unpack_weight(words, scales, fmt):
    g, _, n = scales.shape
    words = np.ascontiguousarray(words).reshape(g, 128, n, -1)
    if fmt == "e4m3":
        vals = words.view(ml_dtypes.float8_e4m3fn).astype(np.float64)
    else:
        nib = np.empty((g, 128, n, 4), np.uint8)
        nib[..., 0::2] = words & 0xF
        nib[..., 1::2] = words >> 4
        vals = E2M1[nib]
    vals = vals * np.repeat(np.exp2(scales.astype(np.float64) - 127.0), 8, axis=1)[..., None]
    return vals.transpose(0, 1, 3, 2).reshape(g * 512, n)


def gelu(v):
    return 0.5 * v * (1.0 + np.tanh(np.sqrt(2.0 / np.pi) * (v + 0.044715 * v**3)))


def striped8(idx):
    return np.concatenate([v.reshape(-1, 16).T for v in idx]).astype(np.uint16)


def unstriped8(offs):
    return np.stack([offs[16 * g:16 * g + 16].T.reshape(-1) for g in range(8)]).astype(np.int64)


def heads(h, wgt, idx8):
    r = np.arange(h.shape[0])
    return wgt[r // 4 % 128] * h[r[:, None], idx8[r % 512 // 64]]


def bf(x):
    return np.asarray(x, np.float32).astype(ml_dtypes.bfloat16)


def planes(Y):
    n, m = Y.shape
    b = f64(bf(Y)).reshape(n // 32, 32, m)
    amax = np.abs(b).max(1)
    byte = np.clip(np.where(amax > 0, np.frexp(amax)[1] - 1 + 127 - 7, 1), 1, 254)
    codes = (b * np.exp2(127.0 - byte)[:, None, :]).reshape(n, m).astype(np.float32).astype(ml_dtypes.float8_e4m3fn).view(np.uint8)
    words = codes.reshape(n // 512, 128, 4, m).transpose(0, 1, 3, 2)
    return np.ascontiguousarray(words), np.ascontiguousarray(byte.astype(np.uint8).reshape(n // 512, 16, m))


K, H, N, T, S, P = 1024, 1024, 512, 4096, 1024, 512

def setup_inputs():
    n = np.random.standard_normal
    s = mx_kscale(K)[:, None]
    u = mx_kscale(H)[:, None]
    tab_words, tab_scales = pack_weight(n((K, T)) * s, "e4m3")
    wp_words, wp_scales = pack_weight(0.8 * n((H, N)) / np.sqrt(H) / u**2, "e2m1")
    return {
        "tab_words": tab_words,
        "tab_scales": tab_scales,
        "offs": striped(np.random.permutation(T)[:S]),
        "offs2": striped8(np.stack([np.random.permutation(S)[:P] for _ in range(8)])),
        "offs3": striped8(np.stack([np.random.permutation(S)[:P] for _ in range(8)])),
        "w1": (1.3 * n((K, H)) / np.sqrt(K) / s).astype(np.float32),
        "b1": (0.5 * n(H)).astype(np.float32),
        "gain": (np.exp(0.3 * n(H)) * u[:, 0]).astype(np.float32),
        "wga": np.repeat(np.random.uniform(0.5, 2.0, (8, P)), 16, axis=0).astype(np.float32),
        "wgb": np.repeat(np.random.uniform(0.5, 2.0, (8, P)), 16, axis=0).astype(np.float32),
        "ws": (0.6 * n((H, N)) / np.sqrt(H) / u).astype(np.float32),
        "wp_words": wp_words,
        "wp_scales": wp_scales,
        "go": np.exp(0.8 * n(N)).astype(np.float32),
    }

def reference(tab_words, tab_scales, offs, offs2, offs3, w1, b1, gain, wga, wgb, ws, wp_words, wp_scales, go):
    v = unpack_weight(tab_words, tab_scales, "e4m3")[:, unstriped(offs)]
    h = f64(gain)[:, None] * np.tanh((mxq(f64(w1), 0, "e4m3").T @ v) + f64(b1)[:, None])
    xa = heads(h, f64(wga), unstriped8(offs2))
    xb = heads(h, f64(wgb), unstriped8(offs3))
    xs = mxq(xa + xb, 0, "e4m3")
    xp = mxq(xa * xb, 0, "e4m3")
    wp = unpack_weight(wp_words, wp_scales, "e2m1")
    y = f64(go)[:, None] * (mxq(f64(ws), 0, "e4m3").T @ xs + wp.T @ xp)
    words, scales = planes(y)
    return y, words, scales

@@ -1,0 +1,255 @@
+from contextlib import ExitStack
+
+import concourse.mybir as mybir
+
+K, H, N, T, S, M = 1024, 1024, 512, 4096, 1024, 512
+FLOPS = 2 * K * H * S + 2 * 2 * H * N * M
+
+F32 = mybir.dt.float32
+BF16 = mybir.dt.bfloat16
+I32 = mybir.dt.int32
+U32 = mybir.dt.uint32
+U16 = mybir.dt.uint16
+U8 = mybir.dt.uint8
+FP8X4 = mybir.dt.float8_e4m3fn_x4
+FP4X4 = mybir.dt.float4_e2m1fn_x4
+ACT = mybir.ActivationFunctionType
+ALU = mybir.AluOpType
+
+P = 128
+PACK = 4
+PASS = P * PACK
+BANK = 512
+PART = 256
+
+
+def tile_list_knockout_epistasis_features_kernel(
+    tc, tab_words, tab_scales, offs, offs2, offs3, w1, b1, gain, wga, wgb, ws, wp_words, wp_scales, go, out_0, out_1, out_2
+):
+    nc = tc.nc
+    with ExitStack() as ctx:
+        keep = ctx.enter_context(tc.tile_pool(name="keep", bufs=1))
+        ring = ctx.enter_context(tc.tile_pool(name="ring", bufs=2))
+        hring = ctx.enter_context(tc.tile_pool(name="hring", bufs=4))
+        psum = ctx.enter_context(tc.psum_pool(name="psum", bufs=1))
+
+        def kept(shape, dtype, name):
+            return keep.tile(shape, dtype, name=name, align_bytes=64)
+
+        tab_sc = kept([P, T], U8, "tab_sc")
+        wp_sc_raw = kept([P, 2, N], U8, "wp_sc_raw")
+        nc.vector.memset(tab_sc[:].bitcast(I32), 0)
+        nc.vector.memset(wp_sc_raw[:].rearrange("p a c -> p (a c)").bitcast(I32), 0)
+
+        list1 = keep.tile([P, S // 16], U16, name="list1")
+        list2 = keep.tile([P, M // 16], U16, name="list2")
+        list3 = keep.tile([P, M // 16], U16, name="list3")
+
+        def load_weight(w, rows, cols, name):
+            raw = kept([P, PACK, PASS], F32, name)
+            nc.sync.dma_start(out=raw[:], in_=w[rows * PASS : (rows + 1) * PASS, cols * PASS : (cols + 1) * PASS].rearrange("(p j) c -> p j c", j=PACK))
+            return raw
+
+        bias = kept([P, 2, 8], F32, "bias")
+        gains = kept([P, 2, 8], F32, "gains")
+        out_gain = kept([P, PACK], F32, "out_gain")
+
+        def load_table(a):
+            words = kept([P, T], I32, "tab%d" % a)
+            nc.sync.dma_start(out=words[:], in_=tab_words[a].rearrange("p t i -> p (t i)").bitcast(I32))
+            return words
+
+        w1_raw = {}
+        for a in range(2):
+            w1_raw[a, 0] = load_weight(w1, a, 0, "w1_raw%d0" % a)
+        tab = [load_table(0)]
+        nc.sync.dma_start(list1[:], offs)
+        for q in range(4):
+            nc.scalar.dma_start(
+                out=tab_sc[32 * q : 32 * q + 8, :].bitcast(I32),
+                in_=tab_scales[:, 4 * q : 4 * q + 4, :].bitcast(I32),
+            )
+        tab.append(load_table(1))
+        nc.sync.dma_start(out=bias[:, :, 0:PACK], in_=b1.rearrange("(b p i) -> p b i", b=2, i=PACK))
+        nc.sync.dma_start(out=gains[:, :, 0:PACK], in_=gain.rearrange("(b p i) -> p b i", b=2, i=PACK))
+        nc.sync.dma_start(list2[:], offs2)
+        nc.sync.dma_start(list3[:], offs3)
+        wa = kept([P, M], F32, "wa")
+        wb = kept([P, M], F32, "wb")
+        nc.sync.dma_start(out=wa[:], in_=wga)
+        nc.sync.dma_start(out=wb[:], in_=wgb)
+        wp_raw = kept([P, 2, 2 * N], U8, "wp_raw")
+        nc.sync.dma_start(out=wp_raw[:].bitcast(I32), in_=wp_words.rearrange("a p c -> p a c").bitcast(I32))
+        for q in range(4):
+            nc.sync.dma_start(
+                out=wp_sc_raw[32 * q : 32 * q + 4, :, :].bitcast(I32),
+                in_=wp_scales[:, 4 * q : 4 * q + 4, :].rearrange("a r c -> r a c").bitcast(I32),
+            )
+        for a in range(2):
+            w1_raw[a, 1] = load_weight(w1, a, 1, "w1_raw%d1" % a)
+        ws_raw = [load_weight(ws, b, 0, "ws_raw%d" % b) for b in range(2)]
+        nc.sync.dma_start(out=out_gain[:], in_=go.rearrange("(p t) -> p t", t=PACK))
+
+        def staging(tag, width):
+            return keep.tile([P, PACK * width], BF16, name="staging", tag=tag, align_bytes=64)
+
+        def quantize_weight(raw, name, tag):
+            grouped = staging(tag, PASS)
+            nc.scalar.activation(
+                out=grouped[:].rearrange("p (t q j) -> p q j t", t=PACK, j=PACK),
+                in_=raw[:].rearrange("p j (q t) -> p q j t", t=PACK),
+                func=ACT.Copy,
+            )
+            codes = kept([P, PASS], U32, name + "_codes")
+            scales = kept([P, PASS], U8, name + "_scales")
+            nc.vector.quantize_mx(out=codes[:].bitcast(FP8X4), scales=scales[:], in_=grouped[:])
+            return codes, scales
+
+        w1_q = {}
+        for a in range(2):
+            w1_q[a, 0] = quantize_weight(w1_raw[a, 0], "w1q%d0" % a, "stage%d" % a)
+
+        v_sc = kept([P, S], U8, "v_sc")
+        nc.vector.tensor_copy(out=v_sc[:], in_=tab_sc[:].indirect(list1[:]))
+        v_words = {}
+        for a in range(2):
+            for half in range(2):
+                picked = kept([P, BANK], U32, "v%d%d" % (a, half))
+                nc.vector.tensor_copy(out=picked[:], in_=tab[a][:].bitcast(U32).indirect(list1[:, 32 * half : 32 * half + 32]))
+                v_words[a, half] = picked
+
+        wp_codes = kept([P, 2, 2 * N], U8, "wp_codes")
+        wp_sc = kept([P, 2, N], U8, "wp_sc")
+        nc.vector.tensor_copy(
+            out=wp_codes[:].bitcast(U16).rearrange("p a (t q) -> p a t q", t=PACK),
+            in_=wp_raw[:].bitcast(U16).rearrange("p a (q t) -> p a t q", t=PACK),
+        )
+        nc.vector.tensor_copy(
+            out=wp_sc[:].rearrange("p a (t q) -> p a t q", t=PACK),
+            in_=wp_sc_raw[:].rearrange("p a (q t) -> p a t q", t=PACK),
+        )
+
+        def profile(b, i):
+            bounded = ring.tile([P, S], F32, name="bounded")
+            for half in range(2):
+                acc = psum.tile([P, BANK], F32, name="acc", tag="bank%d%d" % (i, half))
+                for a in range(2):
+                    codes, scales = w1_q[a, b]
+                    nc.tensor.matmul_mx(
+                        out=acc[:],
+                        lhsT=codes[:, P * i : P * (i + 1)].bitcast(FP8X4),
+                        lhsT_scale=scales[:, P * i : P * (i + 1)],
+                        rhs=v_words[a, half][:].bitcast(FP8X4),
+                        rhs_scale=v_sc[4 * a :, BANK * half : BANK * (half + 1)],
+                        start=(a == 0),
+                        stop=(a == 1),
+                    )
+                nc.scalar.activation(
+                    out=bounded[:, BANK * half : BANK * (half + 1)], in_=acc[:], func=ACT.Tanh, bias=bias[:, b, i : i + 1]
+                )
+            h = hring.tile([P, S], F32, name="h")
+            if (b, i) == (0, 0):
+                for half in range(2):
+                    cols = slice(BANK * half, BANK * (half + 1))
+                    nc.vector.tensor_scalar_mul(h[:, cols], bounded[:, cols], gains[:, b, i : i + 1])
+            else:
+                nc.scalar.activation(out=h[:], in_=bounded[:], func=ACT.Copy, scale=gains[:, b, i : i + 1])
+            return h
+
+        def pick(h, i, xa, xb, m0, width):
+            cols = slice(m0 // 16, (m0 + width) // 16)
+            nc.vector.tensor_tensor(xa[:, i, m0 : m0 + width], h[:].indirect(list2[:, cols]), wa[:, m0 : m0 + width], ALU.mult)
+            nc.vector.tensor_tensor(xb[:, i, m0 : m0 + width], h[:].indirect(list3[:, cols]), wb[:, m0 : m0 + width], ALU.mult)
+
+        def combine(xa, xb, m0, width, name, tags):
+            result = []
+            rounded = []
+            for op, tag in zip((ALU.add, ALU.mult), tags):
+                x = staging(tag, width)
+                nc.vector.tensor_tensor(
+                    x[:].rearrange("p (c e i) -> p c i e", e=2, i=PACK),
+                    xa[:, :, m0 : m0 + width].rearrange("p i (c e) -> p c i e", e=2),
+                    xb[:, :, m0 : m0 + width].rearrange("p i (c e) -> p c i e", e=2),
+                    op,
+                )
+                rounded.append(x)
+            for x, tag in zip(rounded, ("xs", "xp")):
+                codes = kept([P, width], U32, name + tag + "_codes")
+                scales = kept([P, width], U8, name + tag + "_scales")
+                nc.vector.quantize_mx(out=codes[:].bitcast(FP8X4), scales=scales[:], in_=x[:])
+                result.append((codes, scales))
+            return result
+
+
+        def second_stage(b, part, quantised, c0):
+            (xs_codes, xs_scales), (xp_codes, xp_scales) = quantised
+            ws_codes, ws_scales = ws_q[b]
+            cols = slice(c0, c0 + PART)
+            for t in range(PACK):
+                nc.tensor.matmul_mx(
+                    out=sums[part][t // 2][:, t % 2, :],
+                    lhsT=ws_codes[:, P * t : P * (t + 1)].bitcast(FP8X4),
+                    lhsT_scale=ws_scales[:, P * t : P * (t + 1)],
+                    rhs=xs_codes[:, cols].bitcast(FP8X4),
+                    rhs_scale=xs_scales[:, cols],
+                    start=(b == 0 and t % 2 == 0),
+                    stop=False,
+                )
+            for t in range(PACK):
+                nc.tensor.matmul_mx(
+                    out=sums[part][t // 2][:, t % 2, :],
+                    lhsT=wp_codes[:, b, 2 * P * t : 2 * P * (t + 1)].bitcast(FP4X4),
+                    lhsT_scale=wp_sc[:, b, P * t : P * (t + 1)],
+                    rhs=xp_codes[:, cols].bitcast(FP8X4),
+                    rhs_scale=xp_scales[:, cols],
+                    start=False,
+                    stop=(b == 1 and t % 2 == 1),
+                )
+
+        y_scales = kept([P, M], U8, "y_scales")
+
+        def finish(part):
+            last = part == 1
+            cols = slice(part * PART, (part + 1) * PART)
+            y = kept([P, PACK, PART], F32, "y%d" % part)
+            for t in range(PACK):
+                acc = sums[part][t // 2][:, t % 2, :]
+                if last and t >= 2:
+                    nc.vector.tensor_scalar_mul(y[:, t, :], acc, out_gain[:, t : t + 1])
+                else:
+                    nc.scalar.activation(out=y[:, t, :], in_=acc, func=ACT.Copy, scale=out_gain[:, t : t + 1])
+            nc.sync.dma_start(out=out_0.rearrange("(p t) m -> p t m", t=PACK)[:, :, cols], in_=y[:])
+            y_bf = kept([P, PACK * PART], BF16, "y_bf%d" % part)
+            copy = nc.vector.tensor_copy if last else nc.scalar.copy
+            copy(out=y_bf[:].rearrange("p (c e t) -> p c t e", e=2, t=PACK), in_=y[:].rearrange("p t (c e) -> p c t e", e=2))
+            y_codes = kept([P, PART], I32, "y_codes%d" % part)
+            nc.vector.quantize_mx(out=y_codes[:].bitcast(FP8X4), scales=y_scales[:, cols], in_=y_bf[:])
+            nc.sync.dma_start(out=out_1[0].rearrange("p m t -> p (m t)").bitcast(I32)[:, cols], in_=y_codes[:])
+
+        xa = kept([P, PACK, M], F32, "xa0")
+        xb = kept([P, PACK, M], F32, "xb0")
+        for i in range(PACK):
+            pick(profile(0, i), i, xa, xb, 0, M)
+        for a in range(2):
+            w1_q[a, 1] = quantize_weight(w1_raw[a, 1], "w1q%d1" % a, "stage%d" % a)
+        first = combine(xa, xb, 0, M, "b0", ("stage0", "stage1"))
+
+        xa = kept([P, PACK, M], F32, "xa1")
+        xb = kept([P, PACK, M], F32, "xb1")
+        for i in range(PACK - 1):
+            pick(profile(1, i), i, xa, xb, 0, M)
+        h_last = profile(1, PACK - 1)
+        pick(h_last, PACK - 1, xa, xb, 0, PART)
+        ws_q = [quantize_weight(ws_raw[b], "wsq%d" % b, "stage_ws%d" % b) for b in range(2)]
+        sums = [[psum.tile([P, 2, PART], F32, name="sums", tag="bank%d%d" % (part, u)) for u in range(2)] for part in range(2)]
+        for part in range(2):
+            second_stage(0, part, first, part * PART)
+        second_stage(1, 0, combine(xa, xb, 0, PART, "b10", ("stage0", "stage1")), 0)
+        pick(h_last, PACK - 1, xa, xb, PART, PART)
+        last_part = combine(xa, xb, PART, PART, "b11", ("stage2", "stage3"))
+        finish(0)
+        second_stage(1, 1, last_part, 0)
+        finish(1)
+        for q in range(4):
+            queue = nc.sync if q % 2 == 0 else nc.scalar
+            queue.dma_start(out=out_2[0, 4 * q : 4 * q + 4, :].bitcast(I32), in_=y_scales[32 * q : 32 * q + 4, :].bitcast(I32))

@@ -38,7 +38,8 @@ def tile_list_knockout_epistasis_features_kernel(
 
         tab_sc = kept([P, T], U8, "tab_sc")
         wp_sc_raw = kept([P, 2, N], U8, "wp_sc_raw")
-        nc.vector.memset(tab_sc[:].bitcast(I32), 0)
+        nc.vector.memset(tab_sc[:].bitcast(I32)[:, 0:704], 0)
+        nc.gpsimd.memset(tab_sc[:].bitcast(I32)[:, 704:], 0)
         nc.vector.memset(wp_sc_raw[:].rearrange("p a c -> p (a c)").bitcast(I32), 0)
 
         list1 = keep.tile([P, S // 16], U16, name="list1")
@@ -55,36 +56,35 @@ def tile_list_knockout_epistasis_features_kernel(
         out_gain = kept([P, PACK], F32, "out_gain")
 
         def load_table(a):
-            words = kept([P, T], I32, "tab%d" % a)
+            words = keep.tile([P, T], I32, name="tab", tag="tab%d" % a, align_bytes=64)
             nc.sync.dma_start(out=words[:], in_=tab_words[a].rearrange("p t i -> p (t i)").bitcast(I32))
             return words
 
-        w1_raw = {}
-        for a in range(2):
-            w1_raw[a, 0] = load_weight(w1, a, 0, "w1_raw%d0" % a)
-        tab = [load_table(0)]
         nc.sync.dma_start(list1[:], offs)
+        w1_raw = {(0, 0): load_weight(w1, 0, 0, "w1_raw00")}
+        nc.sync.dma_start(out=bias[:, :, 0:PACK], in_=b1.rearrange("(b p i) -> p b i", b=2, i=PACK))
+        nc.sync.dma_start(out=gains[:, :, 0:PACK], in_=gain.rearrange("(b p i) -> p b i", b=2, i=PACK))
         for q in range(4):
-            nc.scalar.dma_start(
+            nc.sync.dma_start(
                 out=tab_sc[32 * q : 32 * q + 8, :].bitcast(I32),
                 in_=tab_scales[:, 4 * q : 4 * q + 4, :].bitcast(I32),
             )
-        tab.append(load_table(1))
-        nc.sync.dma_start(out=bias[:, :, 0:PACK], in_=b1.rearrange("(b p i) -> p b i", b=2, i=PACK))
-        nc.sync.dma_start(out=gains[:, :, 0:PACK], in_=gain.rearrange("(b p i) -> p b i", b=2, i=PACK))
+        w1_raw[1, 0] = load_weight(w1, 1, 0, "w1_raw10")
+        tab = [load_table(0)]
         nc.sync.dma_start(list2[:], offs2)
         nc.sync.dma_start(list3[:], offs3)
-        wa = kept([P, M], F32, "wa")
-        wb = kept([P, M], F32, "wb")
-        nc.sync.dma_start(out=wa[:], in_=wga)
-        nc.sync.dma_start(out=wb[:], in_=wgb)
-        wp_raw = kept([P, 2, 2 * N], U8, "wp_raw")
-        nc.sync.dma_start(out=wp_raw[:].bitcast(I32), in_=wp_words.rearrange("a p c -> p a c").bitcast(I32))
+        tab.append(load_table(1))
         for q in range(4):
             nc.sync.dma_start(
                 out=wp_sc_raw[32 * q : 32 * q + 4, :, :].bitcast(I32),
                 in_=wp_scales[:, 4 * q : 4 * q + 4, :].rearrange("a r c -> r a c").bitcast(I32),
             )
+        wa = kept([P, M], F32, "wa")
+        wb = kept([P, M], F32, "wb")
+        wp_raw = kept([P, 2, 2 * N], U8, "wp_raw")
+        nc.sync.dma_start(out=wa[:], in_=wga)
+        nc.sync.dma_start(out=wp_raw[:].bitcast(I32), in_=wp_words.rearrange("a p c -> p a c").bitcast(I32))
+        nc.sync.dma_start(out=wb[:], in_=wgb)
         for a in range(2):
             w1_raw[a, 1] = load_weight(w1, a, 1, "w1_raw%d1" % a)
         ws_raw = [load_weight(ws, b, 0, "ws_raw%d" % b) for b in range(2)]
@@ -118,14 +118,15 @@ def tile_list_knockout_epistasis_features_kernel(
                 nc.vector.tensor_copy(out=picked[:], in_=tab[a][:].bitcast(U32).indirect(list1[:, 32 * half : 32 * half + 32]))
                 v_words[a, half] = picked
 
-        wp_codes = kept([P, 2, 2 * N], U8, "wp_codes")
-        wp_sc = kept([P, 2, N], U8, "wp_sc")
+        wp_dealt = keep.tile([P, 6 * N], U8, name="wp_dealt", tag="tab1", align_bytes=64)
+        wp_codes = wp_dealt[:, 0 : 4 * N].rearrange("p (a c) -> p a c", a=2)
+        wp_sc = wp_dealt[:, 4 * N : 6 * N].rearrange("p (a c) -> p a c", a=2)
         nc.vector.tensor_copy(
-            out=wp_codes[:].bitcast(U16).rearrange("p a (t q) -> p a t q", t=PACK),
+            out=wp_codes.bitcast(U16).rearrange("p a (t q) -> p a t q", t=PACK),
             in_=wp_raw[:].bitcast(U16).rearrange("p a (q t) -> p a t q", t=PACK),
         )
         nc.vector.tensor_copy(
-            out=wp_sc[:].rearrange("p a (t q) -> p a t q", t=PACK),
+            out=wp_sc.rearrange("p a (t q) -> p a t q", t=PACK),
             in_=wp_sc_raw[:].rearrange("p a (q t) -> p a t q", t=PACK),
         )
 

from contextlib import ExitStack

import concourse.mybir as mybir

K, H, N, T, S, M = 1024, 1024, 512, 4096, 1024, 512
FLOPS = 2 * K * H * S + 2 * 2 * H * N * M

F32 = mybir.dt.float32
BF16 = mybir.dt.bfloat16
I32 = mybir.dt.int32
U32 = mybir.dt.uint32
U16 = mybir.dt.uint16
U8 = mybir.dt.uint8
FP8X4 = mybir.dt.float8_e4m3fn_x4
FP4X4 = mybir.dt.float4_e2m1fn_x4
ACT = mybir.ActivationFunctionType
ALU = mybir.AluOpType

P = 128
PACK = 4
PASS = P * PACK
BANK = 512
PART = 256


def tile_list_knockout_epistasis_features_kernel(
    tc, tab_words, tab_scales, offs, offs2, offs3, w1, b1, gain, wga, wgb, ws, wp_words, wp_scales, go, out_0, out_1, out_2
):
    nc = tc.nc
    with ExitStack() as ctx:
        keep = ctx.enter_context(tc.tile_pool(name="keep", bufs=1))
        ring = ctx.enter_context(tc.tile_pool(name="ring", bufs=2))
        hring = ctx.enter_context(tc.tile_pool(name="hring", bufs=4))
        psum = ctx.enter_context(tc.psum_pool(name="psum", bufs=1))

        def kept(shape, dtype, name):
            return keep.tile(shape, dtype, name=name, align_bytes=64)

        tab_sc = kept([P, T], U8, "tab_sc")
        wp_sc_raw = kept([P, 2, N], U8, "wp_sc_raw")
        nc.vector.memset(tab_sc[:].bitcast(I32)[:, 0:704], 0)
        nc.gpsimd.memset(tab_sc[:].bitcast(I32)[:, 704:], 0)
        nc.vector.memset(wp_sc_raw[:].rearrange("p a c -> p (a c)").bitcast(I32), 0)

        list1 = keep.tile([P, S // 16], U16, name="list1")
        list2 = keep.tile([P, M // 16], U16, name="list2")
        list3 = keep.tile([P, M // 16], U16, name="list3")

        def load_weight(w, rows, cols, name):
            raw = kept([P, PACK, PASS], F32, name)
            nc.sync.dma_start(out=raw[:], in_=w[rows * PASS : (rows + 1) * PASS, cols * PASS : (cols + 1) * PASS].rearrange("(p j) c -> p j c", j=PACK))
            return raw

        bias = kept([P, 2, 8], F32, "bias")
        gains = kept([P, 2, 8], F32, "gains")
        out_gain = kept([P, PACK], F32, "out_gain")

        def load_table(a):
            words = keep.tile([P, T], I32, name="tab", tag="tab%d" % a, align_bytes=64)
            nc.sync.dma_start(out=words[:], in_=tab_words[a].rearrange("p t i -> p (t i)").bitcast(I32))
            return words

        nc.sync.dma_start(list1[:], offs)
        w1_raw = {(0, 0): load_weight(w1, 0, 0, "w1_raw00")}
        nc.sync.dma_start(out=bias[:, :, 0:PACK], in_=b1.rearrange("(b p i) -> p b i", b=2, i=PACK))
        nc.sync.dma_start(out=gains[:, :, 0:PACK], in_=gain.rearrange("(b p i) -> p b i", b=2, i=PACK))
        for q in range(4):
            nc.sync.dma_start(
                out=tab_sc[32 * q : 32 * q + 8, :].bitcast(I32),
                in_=tab_scales[:, 4 * q : 4 * q + 4, :].bitcast(I32),
            )
        w1_raw[1, 0] = load_weight(w1, 1, 0, "w1_raw10")
        tab = [load_table(0)]
        nc.sync.dma_start(list2[:], offs2)
        nc.sync.dma_start(list3[:], offs3)
        tab.append(load_table(1))
        for q in range(4):
            nc.sync.dma_start(
                out=wp_sc_raw[32 * q : 32 * q + 4, :, :].bitcast(I32),
                in_=wp_scales[:, 4 * q : 4 * q + 4, :].rearrange("a r c -> r a c").bitcast(I32),
            )
        wa = kept([P, M], F32, "wa")
        wb = kept([P, M], F32, "wb")
        wp_raw = kept([P, 2, 2 * N], U8, "wp_raw")
        nc.sync.dma_start(out=wa[:], in_=wga)
        nc.sync.dma_start(out=wp_raw[:].bitcast(I32), in_=wp_words.rearrange("a p c -> p a c").bitcast(I32))
        nc.sync.dma_start(out=wb[:], in_=wgb)
        for a in range(2):
            w1_raw[a, 1] = load_weight(w1, a, 1, "w1_raw%d1" % a)
        ws_raw = [load_weight(ws, b, 0, "ws_raw%d" % b) for b in range(2)]
        nc.sync.dma_start(out=out_gain[:], in_=go.rearrange("(p t) -> p t", t=PACK))

        def staging(tag, width):
            return keep.tile([P, PACK * width], BF16, name="staging", tag=tag, align_bytes=64)

        def quantize_weight(raw, name, tag):
            grouped = staging(tag, PASS)
            nc.scalar.activation(
                out=grouped[:].rearrange("p (t q j) -> p q j t", t=PACK, j=PACK),
                in_=raw[:].rearrange("p j (q t) -> p q j t", t=PACK),
                func=ACT.Copy,
            )
            codes = kept([P, PASS], U32, name + "_codes")
            scales = kept([P, PASS], U8, name + "_scales")
            nc.vector.quantize_mx(out=codes[:].bitcast(FP8X4), scales=scales[:], in_=grouped[:])
            return codes, scales

        w1_q = {}
        for a in range(2):
            w1_q[a, 0] = quantize_weight(w1_raw[a, 0], "w1q%d0" % a, "stage%d" % a)

        v_sc = kept([P, S], U8, "v_sc")
        nc.vector.tensor_copy(out=v_sc[:], in_=tab_sc[:].indirect(list1[:]))
        v_words = {}
        for a in range(2):
            for half in range(2):
                picked = kept([P, BANK], U32, "v%d%d" % (a, half))
                nc.vector.tensor_copy(out=picked[:], in_=tab[a][:].bitcast(U32).indirect(list1[:, 32 * half : 32 * half + 32]))
                v_words[a, half] = picked

        wp_dealt = keep.tile([P, 6 * N], U8, name="wp_dealt", tag="tab1", align_bytes=64)
        wp_codes = wp_dealt[:, 0 : 4 * N].rearrange("p (a c) -> p a c", a=2)
        wp_sc = wp_dealt[:, 4 * N : 6 * N].rearrange("p (a c) -> p a c", a=2)
        nc.vector.tensor_copy(
            out=wp_codes.bitcast(U16).rearrange("p a (t q) -> p a t q", t=PACK),
            in_=wp_raw[:].bitcast(U16).rearrange("p a (q t) -> p a t q", t=PACK),
        )
        nc.vector.tensor_copy(
            out=wp_sc.rearrange("p a (t q) -> p a t q", t=PACK),
            in_=wp_sc_raw[:].rearrange("p a (q t) -> p a t q", t=PACK),
        )

        def profile(b, i):
            bounded = ring.tile([P, S], F32, name="bounded")
            for half in range(2):
                acc = psum.tile([P, BANK], F32, name="acc", tag="bank%d%d" % (i, half))
                for a in range(2):
                    codes, scales = w1_q[a, b]
                    nc.tensor.matmul_mx(
                        out=acc[:],
                        lhsT=codes[:, P * i : P * (i + 1)].bitcast(FP8X4),
                        lhsT_scale=scales[:, P * i : P * (i + 1)],
                        rhs=v_words[a, half][:].bitcast(FP8X4),
                        rhs_scale=v_sc[4 * a :, BANK * half : BANK * (half + 1)],
                        start=(a == 0),
                        stop=(a == 1),
                    )
                nc.scalar.activation(
                    out=bounded[:, BANK * half : BANK * (half + 1)], in_=acc[:], func=ACT.Tanh, bias=bias[:, b, i : i + 1]
                )
            h = hring.tile([P, S], F32, name="h")
            if (b, i) == (0, 0):
                for half in range(2):
                    cols = slice(BANK * half, BANK * (half + 1))
                    nc.vector.tensor_scalar_mul(h[:, cols], bounded[:, cols], gains[:, b, i : i + 1])
            else:
                nc.scalar.activation(out=h[:], in_=bounded[:], func=ACT.Copy, scale=gains[:, b, i : i + 1])
            return h

        def pick(h, i, xa, xb, m0, width):
            cols = slice(m0 // 16, (m0 + width) // 16)
            nc.vector.tensor_tensor(xa[:, i, m0 : m0 + width], h[:].indirect(list2[:, cols]), wa[:, m0 : m0 + width], ALU.mult)
            nc.vector.tensor_tensor(xb[:, i, m0 : m0 + width], h[:].indirect(list3[:, cols]), wb[:, m0 : m0 + width], ALU.mult)

        def combine(xa, xb, m0, width, name, tags):
            result = []
            rounded = []
            for op, tag in zip((ALU.add, ALU.mult), tags):
                x = staging(tag, width)
                nc.vector.tensor_tensor(
                    x[:].rearrange("p (c e i) -> p c i e", e=2, i=PACK),
                    xa[:, :, m0 : m0 + width].rearrange("p i (c e) -> p c i e", e=2),
                    xb[:, :, m0 : m0 + width].rearrange("p i (c e) -> p c i e", e=2),
                    op,
                )
                rounded.append(x)
            for x, tag in zip(rounded, ("xs", "xp")):
                codes = kept([P, width], U32, name + tag + "_codes")
                scales = kept([P, width], U8, name + tag + "_scales")
                nc.vector.quantize_mx(out=codes[:].bitcast(FP8X4), scales=scales[:], in_=x[:])
                result.append((codes, scales))
            return result


        def second_stage(b, part, quantised, c0):
            (xs_codes, xs_scales), (xp_codes, xp_scales) = quantised
            ws_codes, ws_scales = ws_q[b]
            cols = slice(c0, c0 + PART)
            for t in range(PACK):
                nc.tensor.matmul_mx(
                    out=sums[part][t // 2][:, t % 2, :],
                    lhsT=ws_codes[:, P * t : P * (t + 1)].bitcast(FP8X4),
                    lhsT_scale=ws_scales[:, P * t : P * (t + 1)],
                    rhs=xs_codes[:, cols].bitcast(FP8X4),
                    rhs_scale=xs_scales[:, cols],
                    start=(b == 0 and t % 2 == 0),
                    stop=False,
                )
            for t in range(PACK):
                nc.tensor.matmul_mx(
                    out=sums[part][t // 2][:, t % 2, :],
                    lhsT=wp_codes[:, b, 2 * P * t : 2 * P * (t + 1)].bitcast(FP4X4),
                    lhsT_scale=wp_sc[:, b, P * t : P * (t + 1)],
                    rhs=xp_codes[:, cols].bitcast(FP8X4),
                    rhs_scale=xp_scales[:, cols],
                    start=False,
                    stop=(b == 1 and t % 2 == 1),
                )

        y_scales = kept([P, M], U8, "y_scales")

        def finish(part):
            last = part == 1
            cols = slice(part * PART, (part + 1) * PART)
            y = kept([P, PACK, PART], F32, "y%d" % part)
            for t in range(PACK):
                acc = sums[part][t // 2][:, t % 2, :]
                if last and t >= 2:
                    nc.vector.tensor_scalar_mul(y[:, t, :], acc, out_gain[:, t : t + 1])
                else:
                    nc.scalar.activation(out=y[:, t, :], in_=acc, func=ACT.Copy, scale=out_gain[:, t : t + 1])
            nc.sync.dma_start(out=out_0.rearrange("(p t) m -> p t m", t=PACK)[:, :, cols], in_=y[:])
            y_bf = kept([P, PACK * PART], BF16, "y_bf%d" % part)
            copy = nc.vector.tensor_copy if last else nc.scalar.copy
            copy(out=y_bf[:].rearrange("p (c e t) -> p c t e", e=2, t=PACK), in_=y[:].rearrange("p t (c e) -> p c t e", e=2))
            y_codes = kept([P, PART], I32, "y_codes%d" % part)
            nc.vector.quantize_mx(out=y_codes[:].bitcast(FP8X4), scales=y_scales[:, cols], in_=y_bf[:])
            nc.sync.dma_start(out=out_1[0].rearrange("p m t -> p (m t)").bitcast(I32)[:, cols], in_=y_codes[:])

        xa = kept([P, PACK, M], F32, "xa0")
        xb = kept([P, PACK, M], F32, "xb0")
        for i in range(PACK):
            pick(profile(0, i), i, xa, xb, 0, M)
        for a in range(2):
            w1_q[a, 1] = quantize_weight(w1_raw[a, 1], "w1q%d1" % a, "stage%d" % a)
        first = combine(xa, xb, 0, M, "b0", ("stage0", "stage1"))

        xa = kept([P, PACK, M], F32, "xa1")
        xb = kept([P, PACK, M], F32, "xb1")
        for i in range(PACK - 1):
            pick(profile(1, i), i, xa, xb, 0, M)
        h_last = profile(1, PACK - 1)
        pick(h_last, PACK - 1, xa, xb, 0, PART)
        ws_q = [quantize_weight(ws_raw[b], "wsq%d" % b, "stage_ws%d" % b) for b in range(2)]
        sums = [[psum.tile([P, 2, PART], F32, name="sums", tag="bank%d%d" % (part, u)) for u in range(2)] for part in range(2)]
        for part in range(2):
            second_stage(0, part, first, part * PART)
        second_stage(1, 0, combine(xa, xb, 0, PART, "b10", ("stage0", "stage1")), 0)
        pick(h_last, PACK - 1, xa, xb, PART, PART)
        last_part = combine(xa, xb, PART, PART, "b11", ("stage2", "stage3"))
        finish(0)
        second_stage(1, 1, last_part, 0)
        finish(1)
        for q in range(4):
            queue = nc.sync if q % 2 == 0 else nc.scalar
            queue.dma_start(out=out_2[0, 4 * q : 4 * q + 4, :].bitcast(I32), in_=y_scales[32 * q : 32 * q + 4, :].bitcast(I32))
